import numpy as np
import ml_dtypes


def mxq(x, axis, fmt="e4m3"):
    dtype, down = {"e4m3": (ml_dtypes.float8_e4m3fn, 7), "e5m2": (ml_dtypes.float8_e5m2, 14)}[fmt]
    v = np.moveaxis(np.asarray(x, np.float32).astype(ml_dtypes.bfloat16).astype(np.float64), axis, -1)
    blocks = v.reshape(v.shape[:-1] + (-1, 32))
    amax = np.abs(blocks).max(-1, keepdims=True)
    byte = np.maximum(np.where(amax > 0, np.frexp(amax)[1] - 1 + 127, 0) - down, 1)
    scale = np.exp2(byte - 127.0)
    codes = (blocks / scale).astype(np.float32).astype(dtype).astype(np.float64)
    return np.moveaxis((codes * scale).reshape(v.shape), -1, axis)


WIDE = False


def mx_kscale(k):
    if not WIDE:
        return np.ones(k)
    levels = np.array([10, -10, 5, -5, 0])
    if k % 512:
        return np.exp2(np.random.permutation(np.resize(levels, k // 32))).repeat(32)
    a = np.empty((k // 512, 16))
    for p in range(k // 512):
        a[p, :8] = np.random.permutation(np.resize(levels, 8))
        for g in range(8):
            far = levels[np.abs(levels - a[p, g]) >= 10]
            a[p, g + 8] = far[np.random.randint(len(far))]
    return np.exp2(a.ravel()).repeat(32)


def f64(x):
    return np.asarray(x).astype(np.float64)


def striped(idx):
    return np.tile(idx.reshape(-1, 16).T, (8, 1)).astype(np.uint16)


def unstriped(offs):
    return offs[:16].T.reshape(-1).astype(np.int64)


def striped8(idx):
    return np.concatenate([x.reshape(-1, 16).T for x in idx]).astype(np.uint16)


def runs(offs, k):
    lists = np.stack([offs[16 * r : 16 * r + 16].T.reshape(-1) for r in range(8)]).astype(np.int64)
    return lists[np.arange(k) % 512 // 64]


def pack_weight(w):
    k, n = w.shape
    w = f64(np.asarray(w, np.float32).astype(ml_dtypes.bfloat16)).reshape(k // 32, 32, n)
    amax = np.abs(w).max(1)
    byte = np.clip(np.where(amax > 0, np.frexp(amax)[1] - 1 + 127 - 7, 1), 1, 254)
    scaled = (w * np.exp2(127.0 - byte)[:, None, :]).reshape(k, n).astype(np.float32)
    words = np.ascontiguousarray(scaled.reshape(k // 512, 128, 4, n).transpose(0, 1, 3, 2)).astype(ml_dtypes.float8_e4m3fn).view(np.uint8)
    return words, np.ascontiguousarray(byte.astype(np.uint8).reshape(k // 512, 16, n))


def unpack_weight(words, scales):
    g, p, n, _ = words.shape
    vals = np.ascontiguousarray(words).view(ml_dtypes.float8_e4m3fn).astype(np.float64) * np.repeat(np.exp2(scales.astype(np.float64) - 127.0), 8, axis=1)[..., None]
    return vals.transpose(0, 1, 3, 2).reshape(g * 512, n)


K, T, S, H, C, U = 512, 2048, 512, 512, 512, 1024


def setup_inputs():
    n = np.random.standard_normal
    s = mx_kscale(K)[:, None]
    packed_xT = pack_weight(n((K, T)) * s)
    return {
        "x_words": packed_xT[0],
        "x_scales": packed_xT[1],
        "w1": (n((K, H)) / np.sqrt(K) / s).astype(np.float32),
        "mem": n((H, U)).astype(np.float32),
        "gs": (np.random.uniform(0.5, 1.5, (K, 1)) / s).astype(np.float32),
        "offs": striped(np.random.permutation(T)[:S]),
        "slot": striped8(np.stack([np.random.permutation(U)[:S] for _ in range(8)])),
        "mate": striped8(np.stack([np.random.permutation(U) for _ in range(8)])),
        "cand": striped(np.random.permutation(T)[:C]),
    }


def reference(x_words, x_scales, w1, mem, gs, offs, slot, mate, cand):
    x_cand = unpack_weight(x_words, x_scales)[:, unstriped(cand)]
    xq = unpack_weight(x_words, x_scales)[:, unstriped(offs)]
    h = mxq(f64(w1), 0, "e4m3").T @ xq
    pg = f64(mem).copy()
    pg[np.arange(H)[:, None], runs(slot, H)] = h
    z = f64(gs) * (pg - (pg[np.arange(H)[:, None], runs(mate, H)]))
    return 0.0625 * ((x_cand.T @ mxq(z, 0, "e4m3")))

@@ -1,0 +1,171 @@
+from contextlib import ExitStack
+
+import concourse.mybir as mybir
+
+K, T, S, H, C, U = 512, 2048, 512, 512, 512, 1024
+FLOPS = 2 * K * H * S + 2 * K * C * U
+
+F32 = mybir.dt.float32
+BF16 = mybir.dt.bfloat16
+I32 = mybir.dt.int32
+U32 = mybir.dt.uint32
+U16 = mybir.dt.uint16
+U8 = mybir.dt.uint8
+FP8X4 = mybir.dt.float8_e4m3fn_x4
+COPY = mybir.ActivationFunctionType.Copy
+SUBTRACT = mybir.AluOpType.subtract
+
+P = 128
+PACK = 4
+GROUP = 16
+CHUNK = 256
+CHUNKS = U // CHUNK
+KIB = 1024
+LAST_SPLIT = 40
+
+
+def tile_picked_candpg_none_p_kernel(tc, x_words, x_scales, w1, mem, gs, offs, slot, mate, cand, out):
+    nc = tc.nc
+    with ExitStack() as ctx:
+        lists = ctx.enter_context(tc.tile_pool(name="lists", bufs=1))
+        keep = ctx.enter_context(tc.tile_pool(name="keep", bufs=1))
+        work = ctx.enter_context(tc.tile_pool(name="work", bufs=1))
+        stage = ctx.enter_context(tc.tile_pool(name="stage", bufs=4))
+        psum = ctx.enter_context(tc.psum_pool(name="psum", bufs=8))
+
+        offs_t = lists.tile([P, S // GROUP], U16, name="offs_t")
+        cand_t = lists.tile([P, C // GROUP], U16, name="cand_t")
+        slot_t = lists.tile([P, S // GROUP], U16, name="slot_t")
+        mate_t = lists.tile([P, U // GROUP], U16, name="mate_t")
+
+        table_words = keep.tile([P, T], I32, name="table_words")
+        table_bytes = keep.tile([P, T], U8, name="table_bytes")
+        w_raw = [work.tile([P, PACK, H // 2], F32, name=f"w_raw{a}", offset=(16 + 4 * a) * KIB, align_bytes=64) for a in range(2)]
+        gain = keep.tile([P, PACK], F32, name="gain")
+        page = [keep.tile([P, U], F32, name=f"page{t}") for t in range(PACK)]
+
+        nc.vector.memset(table_bytes[:].bitcast(I32), 0)
+        nc.sync.dma_start(offs_t[:], offs)
+        nc.sync.dma_start(cand_t[:], cand)
+        w_rows = w1.rearrange("(p j) c -> p j c", j=PACK)
+        nc.sync.dma_start(w_raw[0][:], w_rows[:, :, : H // 2])
+        for q in range(4):
+            nc.sync.dma_start(table_bytes[32 * q : 32 * q + 4, :].bitcast(I32), x_scales[0, 4 * q : 4 * q + 4, :].bitcast(I32))
+        nc.sync.dma_start(w_raw[1][:], w_rows[:, :, H // 2 :])
+        nc.sync.dma_start(table_words[:], x_words[0].rearrange("p n r -> p (n r)").bitcast(I32))
+        mem_rows = mem.rearrange("(p t) w -> p t w", t=PACK)
+        nc.sync.dma_start(slot_t[:], slot)
+        nc.sync.dma_start(page[0][:], mem_rows[:, 0, :])
+        nc.sync.dma_start(gain[:], gs.rearrange("(p t) o -> p (t o)", t=PACK))
+        nc.sync.dma_start(page[1][:], mem_rows[:, 1, :])
+        nc.sync.dma_start(page[2][:], mem_rows[:, 2, :])
+        nc.sync.dma_start(page[3][:], mem_rows[:, 3, :])
+        nc.sync.dma_start(mate_t[:], mate)
+
+        tok_words = work.tile([P, S], U32, name="tok_words", offset=20 * KIB, align_bytes=64)
+        tok_bytes = keep.tile([P, S], U8, name="tok_bytes", align_bytes=64)
+        cand_words = work.tile([P, C], U32, name="cand_words", offset=22 * KIB, align_bytes=64)
+        cand_bytes = keep.tile([P, C], U8, name="cand_bytes", align_bytes=64)
+        nc.vector.tensor_copy(tok_bytes[:], table_bytes[:].indirect(offs_t[:]))
+        nc.vector.tensor_copy(cand_bytes[:], table_bytes[:].indirect(cand_t[:]))
+
+        w_bf = keep.tile([P, PACK * P * PACK], BF16, name="w_bf", align_bytes=64)
+        w_dealt = w_bf[:].rearrange("p (t m j) -> p m j t", t=PACK, j=PACK)
+        for a in range(2):
+            nc.scalar.copy(w_dealt[:, a * (P // 2) : (a + 1) * (P // 2), :, :], w_raw[a][:].rearrange("p j (m t) -> p m j t", t=PACK))
+        w_words = keep.tile([P, H], U32, name="w_words", align_bytes=64)
+        w_bytes = keep.tile([P, H], U8, name="w_bytes", align_bytes=64)
+
+        h_all = work.tile([P, PACK, S], F32, name="h_all", offset=0, align_bytes=64)
+        nc.vector.quantize_mx(out=w_words[:].bitcast(FP8X4), scales=w_bytes[:], in_=w_bf[:])
+        half = S // 2
+        for a in range(2):
+            nc.vector.tensor_copy(tok_words[:, a * half : (a + 1) * half],
+                                  table_words[:].bitcast(U32).indirect(offs_t[:, a * half // GROUP : (a + 1) * half // GROUP]))
+        nc.vector.tensor_copy(cand_words[:], table_words[:].bitcast(U32).indirect(cand_t[:]))
+        for t in range(PACK):
+            cols = slice(t * P, (t + 1) * P)
+            width = half if t == 0 else S
+            for s0 in range(0, S, width):
+                toks = slice(s0, s0 + width)
+                h_bank = psum.tile([P, width], F32, name="h_bank", tag="bank")
+                nc.tensor.matmul_mx(out=h_bank[:], lhsT=w_words[:, cols].bitcast(FP8X4), lhsT_scale=w_bytes[:, cols],
+                                    rhs=tok_words[:, toks].bitcast(FP8X4), rhs_scale=tok_bytes[:, toks], start=True, stop=True)
+                nc.scalar.copy(h_all[:, t, toks], h_bank[:])
+
+        window = [keep.tile([P, U], F32, name=f"window{t}") for t in range(PACK)]
+        plain = [[None] * CHUNKS for t in range(PACK)]
+        for t in range(PACK):
+            nc.vector.tensor_copy(page[t][:].indirect(slot_t[:]), h_all[:, t, :])
+            nc.scalar.activation(window[t][:], page[t][:], COPY, scale=gain[:, t : t + 1])
+            if t < PACK - 1:
+                whole = keep.tile([P, U], F32, name=f"plain{t}")
+                nc.scalar.activation(whole[:], page[t][:], COPY, scale=gain[:, t : t + 1])
+                for c in range(CHUNKS):
+                    plain[t][c] = whole[:, c * CHUNK : (c + 1) * CHUNK]
+            else:
+                first = work.tile([P, CHUNK], F32, name="plain_first", offset=8 * KIB, align_bytes=64)
+                nc.scalar.activation(first[:], page[t][:, :CHUNK], COPY, scale=gain[:, t : t + 1])
+                rest = keep.tile([P, U - CHUNK], F32, name="plain_rest")
+                nc.scalar.activation(rest[:], page[t][:, CHUNK:], COPY, scale=gain[:, t : t + 1])
+                plain[t][0] = first[:]
+                for c in range(1, CHUNKS):
+                    plain[t][c] = rest[:, (c - 1) * CHUNK : c * CHUNK]
+
+        out_rows = out.rearrange("(m q) w -> q m w", q=P)
+        span = PACK * CHUNK
+        diff0 = work.tile([P, span], F32, name="diff0", offset=0, align_bytes=64)
+        diff1 = work.tile([P, span], F32, name="diff1", offset=8 * KIB, align_bytes=64)
+        z_bf0 = work.tile([P, span], BF16, name="z_bf0", offset=12 * KIB, align_bytes=64)
+        late = work.tile([P, span + span // 2], F32, name="late", offset=0, align_bytes=64)
+        z_bf2 = keep.tile([P, span], BF16, name="z_bf2", align_bytes=64)
+        z_bf3 = keep.tile([P, span], BF16, name="z_bf3", align_bytes=64)
+        diffs = [diff0[:], diff1[:], late[:, span // 2 :], late[:, :span]]
+        z_bf = [z_bf0[:], late[:, : span // 2].bitcast(BF16), z_bf2[:], z_bf3[:]]
+
+        def gather(c, planes):
+            per = CHUNK // GROUP
+            for t in planes:
+                nc.vector.tensor_tensor(diffs[c][:, t * CHUNK : (t + 1) * CHUNK],
+                                        window[t][:].indirect(mate_t[:, c * per : (c + 1) * per]), plain[t][c], SUBTRACT)
+
+        def weave(c):
+            dst = z_bf[c].rearrange("p (n i t) -> p n t i", i=4, t=PACK)
+            src = diffs[c].rearrange("p (t n i) -> p n t i", t=PACK, i=4)
+            if c < CHUNKS - 1:
+                nc.scalar.copy(dst, src)
+            else:
+                nc.vector.tensor_copy(dst[:, :LAST_SPLIT], src[:, :LAST_SPLIT])
+                nc.scalar.copy(dst[:, LAST_SPLIT:], src[:, LAST_SPLIT:])
+
+        def score(c):
+            z_words = stage.tile([P, CHUNK], U32, name="z_words", align_bytes=64)
+            z_bytes = stage.tile([P, CHUNK], U8, name="z_bytes", align_bytes=64)
+            nc.vector.quantize_mx(out=z_words[:].bitcast(FP8X4), scales=z_bytes[:], in_=z_bf[c])
+            per_bank = 2 if c < CHUNKS - 1 else 1
+            for b in range(PACK // per_bank):
+                bank = psum.tile([P, per_bank, CHUNK], F32, name="out_bank", tag="bank")
+                for i in range(per_bank):
+                    rows = slice((per_bank * b + i) * P, (per_bank * b + i + 1) * P)
+                    nc.tensor.matmul_mx(out=bank[:, i, :], lhsT=cand_words[:, rows].bitcast(FP8X4), lhsT_scale=cand_bytes[:, rows],
+                                        rhs=z_words[:].bitcast(FP8X4), rhs_scale=z_bytes[:], start=True, stop=True)
+                result = stage.tile([P, per_bank, CHUNK], F32, name="result", bufs=8)
+                if c == CHUNKS - 1 and b % 2 == 1:
+                    nc.vector.tensor_scalar_mul(result[:], bank[:], -0.0625)
+                else:
+                    nc.scalar.activation(result[:], bank[:], COPY, scale=-0.0625)
+                nc.sync.dma_start(out_rows[:, per_bank * b : per_bank * (b + 1), c * CHUNK : (c + 1) * CHUNK], result[:])
+
+        gather(0, range(PACK))
+        weave(0)
+        gather(1, range(PACK))
+        weave(1)
+        score(0)
+        gather(2, range(PACK))
+        weave(2)
+        score(1)
+        gather(3, range(2))
+        score(2)
+        gather(3, range(2, PACK))
+        weave(3)
+        score(3)

@@ -42,7 +42,8 @@ def tile_picked_candpg_none_p_kernel(tc, x_words, x_scales, w1, mem, gs, offs, s
         table_bytes = keep.tile([P, T], U8, name="table_bytes")
         w_raw = [work.tile([P, PACK, H // 2], F32, name=f"w_raw{a}", offset=(16 + 4 * a) * KIB, align_bytes=64) for a in range(2)]
         gain = keep.tile([P, PACK], F32, name="gain")
-        page = [keep.tile([P, U], F32, name=f"page{t}") for t in range(PACK)]
+        page = [keep.tile([P, U], F32, name=f"page{t}") for t in range(PACK - 1)]
+        page.append(work.tile([P, U], F32, name="page_last", offset=8 * KIB, align_bytes=64))
 
         nc.vector.memset(table_bytes[:].bitcast(I32), 0)
         nc.sync.dma_start(offs_t[:], offs)
@@ -76,7 +77,7 @@ def tile_picked_candpg_none_p_kernel(tc, x_words, x_scales, w1, mem, gs, offs, s
         w_words = keep.tile([P, H], U32, name="w_words", align_bytes=64)
         w_bytes = keep.tile([P, H], U8, name="w_bytes", align_bytes=64)
 
-        h_all = work.tile([P, PACK, S], F32, name="h_all", offset=0, align_bytes=64)
+        h_all = keep.tile([P, PACK, S], F32, name="h_all")
         nc.vector.quantize_mx(out=w_words[:].bitcast(FP8X4), scales=w_bytes[:], in_=w_bf[:])
         half = S // 2
         for a in range(2):
@@ -104,10 +105,10 @@ def tile_picked_candpg_none_p_kernel(tc, x_words, x_scales, w1, mem, gs, offs, s
                 for c in range(CHUNKS):
                     plain[t][c] = whole[:, c * CHUNK : (c + 1) * CHUNK]
             else:
-                first = work.tile([P, CHUNK], F32, name="plain_first", offset=8 * KIB, align_bytes=64)
+                first = keep.tile([P, CHUNK], F32, name="plain_first")
                 nc.scalar.activation(first[:], page[t][:, :CHUNK], COPY, scale=gain[:, t : t + 1])
                 rest = keep.tile([P, U - CHUNK], F32, name="plain_rest")
-                nc.scalar.activation(rest[:], page[t][:, CHUNK:], COPY, scale=gain[:, t : t + 1])
+                nc.scalar.copy(rest[:], window[t][:, CHUNK:])
                 plain[t][0] = first[:]
                 for c in range(1, CHUNKS):
                     plain[t][c] = rest[:, (c - 1) * CHUNK : c * CHUNK]
@@ -118,10 +119,11 @@ def tile_picked_candpg_none_p_kernel(tc, x_words, x_scales, w1, mem, gs, offs, s
         diff1 = work.tile([P, span], F32, name="diff1", offset=8 * KIB, align_bytes=64)
         z_bf0 = work.tile([P, span], BF16, name="z_bf0", offset=12 * KIB, align_bytes=64)
         late = work.tile([P, span + span // 2], F32, name="late", offset=0, align_bytes=64)
+        z_bf1 = keep.tile([P, span], BF16, name="z_bf1", align_bytes=64)
         z_bf2 = keep.tile([P, span], BF16, name="z_bf2", align_bytes=64)
         z_bf3 = keep.tile([P, span], BF16, name="z_bf3", align_bytes=64)
         diffs = [diff0[:], diff1[:], late[:, span // 2 :], late[:, :span]]
-        z_bf = [z_bf0[:], late[:, : span // 2].bitcast(BF16), z_bf2[:], z_bf3[:]]
+        z_bf = [z_bf0[:], z_bf1[:], z_bf2[:], z_bf3[:]]
 
         def gather(c, planes):
             per = CHUNK // GROUP

@@ -21,7 +21,7 @@ GROUP = 16
 CHUNK = 256
 CHUNKS = U // CHUNK
 KIB = 1024
-LAST_SPLIT = 40
+LAST_SPLIT = 44
 
 
 def tile_picked_candpg_none_p_kernel(tc, x_words, x_scales, w1, mem, gs, offs, slot, mate, cand, out):
@@ -118,11 +118,11 @@ def tile_picked_candpg_none_p_kernel(tc, x_words, x_scales, w1, mem, gs, offs, s
         diff0 = work.tile([P, span], F32, name="diff0", offset=0, align_bytes=64)
         diff1 = work.tile([P, span], F32, name="diff1", offset=8 * KIB, align_bytes=64)
         z_bf0 = work.tile([P, span], BF16, name="z_bf0", offset=12 * KIB, align_bytes=64)
-        late = work.tile([P, span + span // 2], F32, name="late", offset=0, align_bytes=64)
+        late = work.tile([P, 2 * span - CHUNK], F32, name="late", offset=0, align_bytes=64)
         z_bf1 = keep.tile([P, span], BF16, name="z_bf1", align_bytes=64)
         z_bf2 = keep.tile([P, span], BF16, name="z_bf2", align_bytes=64)
         z_bf3 = keep.tile([P, span], BF16, name="z_bf3", align_bytes=64)
-        diffs = [diff0[:], diff1[:], late[:, span // 2 :], late[:, :span]]
+        diffs = [diff0[:], diff1[:], late[:, span - CHUNK :], late[:, :span]]
         z_bf = [z_bf0[:], z_bf1[:], z_bf2[:], z_bf3[:]]
 
         def gather(c, planes):
@@ -166,8 +166,8 @@ def tile_picked_candpg_none_p_kernel(tc, x_words, x_scales, w1, mem, gs, offs, s
         gather(2, range(PACK))
         weave(2)
         score(1)
-        gather(3, range(2))
+        gather(3, range(3))
         score(2)
-        gather(3, range(2, PACK))
+        gather(3, range(3, PACK))
         weave(3)
         score(3)

@@ -21,7 +21,6 @@ GROUP = 16
 CHUNK = 256
 CHUNKS = U // CHUNK
 KIB = 1024
-LAST_SPLIT = 44
 
 
 def tile_picked_candpg_none_p_kernel(tc, x_words, x_scales, w1, mem, gs, offs, slot, mate, cand, out):
@@ -121,9 +120,8 @@ def tile_picked_candpg_none_p_kernel(tc, x_words, x_scales, w1, mem, gs, offs, s
         late = work.tile([P, 2 * span - CHUNK], F32, name="late", offset=0, align_bytes=64)
         z_bf1 = keep.tile([P, span], BF16, name="z_bf1", align_bytes=64)
         z_bf2 = keep.tile([P, span], BF16, name="z_bf2", align_bytes=64)
-        z_bf3 = keep.tile([P, span], BF16, name="z_bf3", align_bytes=64)
         diffs = [diff0[:], diff1[:], late[:, span - CHUNK :], late[:, :span]]
-        z_bf = [z_bf0[:], z_bf1[:], z_bf2[:], z_bf3[:]]
+        z_bf = [z_bf0[:], z_bf1[:], z_bf2[:]]
 
         def gather(c, planes):
             per = CHUNK // GROUP
@@ -134,17 +132,13 @@ def tile_picked_candpg_none_p_kernel(tc, x_words, x_scales, w1, mem, gs, offs, s
         def weave(c):
             dst = z_bf[c].rearrange("p (n i t) -> p n t i", i=4, t=PACK)
             src = diffs[c].rearrange("p (t n i) -> p n t i", t=PACK, i=4)
-            if c < CHUNKS - 1:
-                nc.scalar.copy(dst, src)
-            else:
-                nc.vector.tensor_copy(dst[:, :LAST_SPLIT], src[:, :LAST_SPLIT])
-                nc.scalar.copy(dst[:, LAST_SPLIT:], src[:, LAST_SPLIT:])
+            nc.scalar.copy(dst, src)
 
         def score(c):
             z_words = stage.tile([P, CHUNK], U32, name="z_words", align_bytes=64)
             z_bytes = stage.tile([P, CHUNK], U8, name="z_bytes", align_bytes=64)
             nc.vector.quantize_mx(out=z_words[:].bitcast(FP8X4), scales=z_bytes[:], in_=z_bf[c])
-            per_bank = 2 if c < CHUNKS - 1 else 1
+            per_bank = 2 if c < CHUNKS - 2 else 1
             for b in range(PACK // per_bank):
                 bank = psum.tile([P, per_bank, CHUNK], F32, name="out_bank", tag="bank")
                 for i in range(per_bank):
@@ -152,10 +146,7 @@ def tile_picked_candpg_none_p_kernel(tc, x_words, x_scales, w1, mem, gs, offs, s
                     nc.tensor.matmul_mx(out=bank[:, i, :], lhsT=cand_words[:, rows].bitcast(FP8X4), lhsT_scale=cand_bytes[:, rows],
                                         rhs=z_words[:].bitcast(FP8X4), rhs_scale=z_bytes[:], start=True, stop=True)
                 result = stage.tile([P, per_bank, CHUNK], F32, name="result", bufs=8)
-                if c == CHUNKS - 1 and b % 2 == 1:
-                    nc.vector.tensor_scalar_mul(result[:], bank[:], -0.0625)
-                else:
-                    nc.scalar.activation(result[:], bank[:], COPY, scale=-0.0625)
+                nc.scalar.activation(result[:], bank[:], COPY, scale=-0.0625)
                 nc.sync.dma_start(out_rows[:, per_bank * b : per_bank * (b + 1), c * CHUNK : (c + 1) * CHUNK], result[:])
 
         gather(0, range(PACK))
@@ -169,5 +160,25 @@ def tile_picked_candpg_none_p_kernel(tc, x_words, x_scales, w1, mem, gs, offs, s
         gather(3, range(3))
         score(2)
         gather(3, range(3, PACK))
-        weave(3)
-        score(3)
+        c = CHUNKS - 1
+        src = diffs[c].rearrange("p (t n i) -> p n t i", t=PACK, i=4)
+        z_half = [keep.tile([P, span // 2], BF16, name=f"z_half{a}", align_bytes=64) for a in range(2)]
+        half_words = [keep.tile([P, CHUNK // 2], U32, name=f"half_words{a}", align_bytes=64) for a in range(2)]
+        half_bytes = [keep.tile([P, CHUNK // 2], U8, name=f"half_bytes{a}", align_bytes=64) for a in range(2)]
+        for a in range(2):
+            nc.vector.tensor_copy(z_half[a][:].rearrange("p (n i t) -> p n t i", i=4, t=PACK), src[:, a * (CHUNK // 8) : (a + 1) * (CHUNK // 8)])
+        for a in range(2):
+            nc.vector.quantize_mx(out=half_words[a][:].bitcast(FP8X4), scales=half_bytes[a][:], in_=z_half[a][:])
+        banks = [psum.tile([P, CHUNK], F32, name=f"last_bank{m}", tag="bank") for m in range(PACK)]
+        for a in range(2):
+            for m in range(PACK):
+                rows = slice(m * P, (m + 1) * P)
+                nc.tensor.matmul_mx(out=banks[m][:, a * (CHUNK // 2) : (a + 1) * (CHUNK // 2)], lhsT=cand_words[:, rows].bitcast(FP8X4), lhsT_scale=cand_bytes[:, rows],
+                                    rhs=half_words[a][:].bitcast(FP8X4), rhs_scale=half_bytes[a][:], start=True, stop=True)
+        for m in range(PACK):
+            result = stage.tile([P, 1, CHUNK], F32, name="result", bufs=8)
+            if m % 2 == 1:
+                nc.vector.tensor_scalar_mul(result[:, 0, :], banks[m][:], -0.0625)
+            else:
+                nc.scalar.activation(result[:, 0, :], banks[m][:], COPY, scale=-0.0625)
+            nc.sync.dma_start(out_rows[:, m : m + 1, c * CHUNK : (c + 1) * CHUNK], result[:])

@@ -17,10 +17,25 @@ SUBTRACT = mybir.AluOpType.subtract
 
 P = 128
 PACK = 4
+QUADRANT = 32
 GROUP = 16
+LINE = 4
 CHUNK = 256
 CHUNKS = U // CHUNK
+SPAN = PACK * CHUNK
+CAND_BLOCKS = C // P
+BANKS = 8
+OUT_FACTOR = -0.0625
 KIB = 1024
+
+AT_DIFFS = 0
+AT_LAST_PAGE = 8 * KIB
+AT_W_SECOND = 12 * KIB
+
+
+def multiply(nc, bank, lhs_words, lhs_bytes, rhs_words, rhs_bytes):
+    nc.tensor.matmul_mx(out=bank, lhsT=lhs_words.bitcast(FP8X4), lhsT_scale=lhs_bytes,
+                        rhs=rhs_words.bitcast(FP8X4), rhs_scale=rhs_bytes, start=True, stop=True)
 
 
 def tile_picked_candpg_none_p_kernel(tc, x_words, x_scales, w1, mem, gs, offs, slot, mate, cand, out):
@@ -28,157 +43,146 @@ def tile_picked_candpg_none_p_kernel(tc, x_words, x_scales, w1, mem, gs, offs, s
     with ExitStack() as ctx:
         lists = ctx.enter_context(tc.tile_pool(name="lists", bufs=1))
         keep = ctx.enter_context(tc.tile_pool(name="keep", bufs=1))
-        work = ctx.enter_context(tc.tile_pool(name="work", bufs=1))
-        stage = ctx.enter_context(tc.tile_pool(name="stage", bufs=4))
-        psum = ctx.enter_context(tc.psum_pool(name="psum", bufs=8))
+        shared = ctx.enter_context(tc.tile_pool(name="shared", bufs=1))
+        stage = ctx.enter_context(tc.tile_pool(name="stage", bufs=CHUNKS))
+        psum = ctx.enter_context(tc.psum_pool(name="psum", bufs=BANKS))
 
         offs_t = lists.tile([P, S // GROUP], U16, name="offs_t")
         cand_t = lists.tile([P, C // GROUP], U16, name="cand_t")
         slot_t = lists.tile([P, S // GROUP], U16, name="slot_t")
         mate_t = lists.tile([P, U // GROUP], U16, name="mate_t")
-
         table_words = keep.tile([P, T], I32, name="table_words")
         table_bytes = keep.tile([P, T], U8, name="table_bytes")
-        w_raw = [work.tile([P, PACK, H // 2], F32, name=f"w_raw{a}", offset=(16 + 4 * a) * KIB, align_bytes=64) for a in range(2)]
+        w_raw = [keep.tile([P, PACK, H // 2], F32, name="w_first"),
+                 shared.tile([P, PACK, H // 2], F32, name="w_second", offset=AT_W_SECOND, align_bytes=64)]
         gain = keep.tile([P, PACK], F32, name="gain")
         page = [keep.tile([P, U], F32, name=f"page{t}") for t in range(PACK - 1)]
-        page.append(work.tile([P, U], F32, name="page_last", offset=8 * KIB, align_bytes=64))
+        page.append(shared.tile([P, U], F32, name="page_last", offset=AT_LAST_PAGE, align_bytes=64))
 
         nc.vector.memset(table_bytes[:].bitcast(I32), 0)
         nc.sync.dma_start(offs_t[:], offs)
         nc.sync.dma_start(cand_t[:], cand)
         w_rows = w1.rearrange("(p j) c -> p j c", j=PACK)
         nc.sync.dma_start(w_raw[0][:], w_rows[:, :, : H // 2])
-        for q in range(4):
-            nc.sync.dma_start(table_bytes[32 * q : 32 * q + 4, :].bitcast(I32), x_scales[0, 4 * q : 4 * q + 4, :].bitcast(I32))
+        scale_rows = x_scales[0].rearrange("(q r) n -> r q n", r=PACK)
+        for r in range(PACK):
+            nc.sync.dma_start(table_bytes[r:P:QUADRANT, :].bitcast(I32), scale_rows[r].bitcast(I32))
         nc.sync.dma_start(w_raw[1][:], w_rows[:, :, H // 2 :])
-        nc.sync.dma_start(table_words[:], x_words[0].rearrange("p n r -> p (n r)").bitcast(I32))
-        mem_rows = mem.rearrange("(p t) w -> p t w", t=PACK)
+        nc.sync.dma_start(table_words[:], x_words[0].rearrange("p n j -> p (n j)").bitcast(I32))
+        mem_planes = mem.rearrange("(p t) w -> p t w", t=PACK)
         nc.sync.dma_start(slot_t[:], slot)
-        nc.sync.dma_start(page[0][:], mem_rows[:, 0, :])
+        nc.sync.dma_start(page[0][:], mem_planes[:, 0, :])
         nc.sync.dma_start(gain[:], gs.rearrange("(p t) o -> p (t o)", t=PACK))
-        nc.sync.dma_start(page[1][:], mem_rows[:, 1, :])
-        nc.sync.dma_start(page[2][:], mem_rows[:, 2, :])
-        nc.sync.dma_start(page[3][:], mem_rows[:, 3, :])
+        for t in range(1, PACK):
+            nc.sync.dma_start(page[t][:], mem_planes[:, t, :])
         nc.sync.dma_start(mate_t[:], mate)
 
-        tok_words = work.tile([P, S], U32, name="tok_words", offset=20 * KIB, align_bytes=64)
+        tok_words = shared.tile([P, S], U32, name="tok_words", offset=AT_W_SECOND, align_bytes=64)
         tok_bytes = keep.tile([P, S], U8, name="tok_bytes", align_bytes=64)
-        cand_words = work.tile([P, C], U32, name="cand_words", offset=22 * KIB, align_bytes=64)
+        cand_words = shared.tile([P, C], U32, name="cand_words", offset=AT_W_SECOND + 4 * S, align_bytes=64)
         cand_bytes = keep.tile([P, C], U8, name="cand_bytes", align_bytes=64)
         nc.vector.tensor_copy(tok_bytes[:], table_bytes[:].indirect(offs_t[:]))
         nc.vector.tensor_copy(cand_bytes[:], table_bytes[:].indirect(cand_t[:]))
 
-        w_bf = keep.tile([P, PACK * P * PACK], BF16, name="w_bf", align_bytes=64)
+        w_bf = keep.tile([P, H * PACK], BF16, name="w_bf", align_bytes=64)
         w_dealt = w_bf[:].rearrange("p (t m j) -> p m j t", t=PACK, j=PACK)
         for a in range(2):
             nc.scalar.copy(w_dealt[:, a * (P // 2) : (a + 1) * (P // 2), :, :], w_raw[a][:].rearrange("p j (m t) -> p m j t", t=PACK))
         w_words = keep.tile([P, H], U32, name="w_words", align_bytes=64)
         w_bytes = keep.tile([P, H], U8, name="w_bytes", align_bytes=64)
-
-        h_all = keep.tile([P, PACK, S], F32, name="h_all")
+        h_planes = keep.tile([P, PACK, S], F32, name="h_planes")
         nc.vector.quantize_mx(out=w_words[:].bitcast(FP8X4), scales=w_bytes[:], in_=w_bf[:])
-        half = S // 2
-        for a in range(2):
-            nc.vector.tensor_copy(tok_words[:, a * half : (a + 1) * half],
-                                  table_words[:].bitcast(U32).indirect(offs_t[:, a * half // GROUP : (a + 1) * half // GROUP]))
+
+        half_s = S // 2
+        for s0 in range(0, S, half_s):
+            nc.vector.tensor_copy(tok_words[:, s0 : s0 + half_s],
+                                  table_words[:].bitcast(U32).indirect(offs_t[:, s0 // GROUP : (s0 + half_s) // GROUP]))
         nc.vector.tensor_copy(cand_words[:], table_words[:].bitcast(U32).indirect(cand_t[:]))
         for t in range(PACK):
             cols = slice(t * P, (t + 1) * P)
-            width = half if t == 0 else S
+            width = half_s if t == 0 else S
             for s0 in range(0, S, width):
                 toks = slice(s0, s0 + width)
                 h_bank = psum.tile([P, width], F32, name="h_bank", tag="bank")
-                nc.tensor.matmul_mx(out=h_bank[:], lhsT=w_words[:, cols].bitcast(FP8X4), lhsT_scale=w_bytes[:, cols],
-                                    rhs=tok_words[:, toks].bitcast(FP8X4), rhs_scale=tok_bytes[:, toks], start=True, stop=True)
-                nc.scalar.copy(h_all[:, t, toks], h_bank[:])
+                multiply(nc, h_bank[:], w_words[:, cols], w_bytes[:, cols], tok_words[:, toks], tok_bytes[:, toks])
+                nc.scalar.copy(h_planes[:, t, toks], h_bank[:])
 
         window = [keep.tile([P, U], F32, name=f"window{t}") for t in range(PACK)]
-        plain = [[None] * CHUNKS for t in range(PACK)]
+        plain = []
         for t in range(PACK):
-            nc.vector.tensor_copy(page[t][:].indirect(slot_t[:]), h_all[:, t, :])
-            nc.scalar.activation(window[t][:], page[t][:], COPY, scale=gain[:, t : t + 1])
+            weight = gain[:, t : t + 1]
+            nc.vector.tensor_copy(page[t][:].indirect(slot_t[:]), h_planes[:, t, :])
+            nc.scalar.activation(window[t][:], page[t][:], COPY, scale=weight)
             if t < PACK - 1:
                 whole = keep.tile([P, U], F32, name=f"plain{t}")
-                nc.scalar.activation(whole[:], page[t][:], COPY, scale=gain[:, t : t + 1])
-                for c in range(CHUNKS):
-                    plain[t][c] = whole[:, c * CHUNK : (c + 1) * CHUNK]
+                nc.scalar.activation(whole[:], page[t][:], COPY, scale=weight)
+                plain.append([whole[:, c * CHUNK : (c + 1) * CHUNK] for c in range(CHUNKS)])
             else:
                 first = keep.tile([P, CHUNK], F32, name="plain_first")
-                nc.scalar.activation(first[:], page[t][:, :CHUNK], COPY, scale=gain[:, t : t + 1])
+                nc.scalar.activation(first[:], page[t][:, :CHUNK], COPY, scale=weight)
                 rest = keep.tile([P, U - CHUNK], F32, name="plain_rest")
                 nc.scalar.copy(rest[:], window[t][:, CHUNK:])
-                plain[t][0] = first[:]
-                for c in range(1, CHUNKS):
-                    plain[t][c] = rest[:, (c - 1) * CHUNK : c * CHUNK]
+                plain.append([first[:]] + [rest[:, c * CHUNK : (c + 1) * CHUNK] for c in range(CHUNKS - 1)])
 
-        out_rows = out.rearrange("(m q) w -> q m w", q=P)
-        span = PACK * CHUNK
-        diff0 = work.tile([P, span], F32, name="diff0", offset=0, align_bytes=64)
-        diff1 = work.tile([P, span], F32, name="diff1", offset=8 * KIB, align_bytes=64)
-        z_bf0 = work.tile([P, span], BF16, name="z_bf0", offset=12 * KIB, align_bytes=64)
-        late = work.tile([P, 2 * span - CHUNK], F32, name="late", offset=0, align_bytes=64)
-        z_bf1 = keep.tile([P, span], BF16, name="z_bf1", align_bytes=64)
-        z_bf2 = keep.tile([P, span], BF16, name="z_bf2", align_bytes=64)
-        diffs = [diff0[:], diff1[:], late[:, span - CHUNK :], late[:, :span]]
-        z_bf = [z_bf0[:], z_bf1[:], z_bf2[:]]
+        diff0 = shared.tile([P, SPAN], F32, name="diff0", offset=AT_DIFFS, align_bytes=64)
+        diff1 = shared.tile([P, SPAN], F32, name="diff1", offset=AT_LAST_PAGE, align_bytes=64)
+        diff23 = shared.tile([P, 2 * SPAN - CHUNK], F32, name="diff23", offset=AT_DIFFS, align_bytes=64)
+        diffs = [diff0[:], diff1[:], diff23[:, SPAN - CHUNK :], diff23[:, :SPAN]]
+        z_bf = [keep.tile([P, SPAN], BF16, name=f"z_bf{c}", align_bytes=64) for c in range(CHUNKS - 1)]
+        out_blocks = out.rearrange("(m q) w -> q m w", q=P)
 
         def gather(c, planes):
-            per = CHUNK // GROUP
+            entries = mate_t[:, c * CHUNK // GROUP : (c + 1) * CHUNK // GROUP]
             for t in planes:
-                nc.vector.tensor_tensor(diffs[c][:, t * CHUNK : (t + 1) * CHUNK],
-                                        window[t][:].indirect(mate_t[:, c * per : (c + 1) * per]), plain[t][c], SUBTRACT)
+                nc.vector.tensor_tensor(diffs[c][:, t * CHUNK : (t + 1) * CHUNK], window[t][:].indirect(entries), plain[t][c], SUBTRACT)
 
-        def weave(c):
-            dst = z_bf[c].rearrange("p (n i t) -> p n t i", i=4, t=PACK)
-            src = diffs[c].rearrange("p (t n i) -> p n t i", t=PACK, i=4)
-            nc.scalar.copy(dst, src)
+        def by_lines(c):
+            return diffs[c].rearrange("p (t n i) -> p n t i", t=PACK, i=LINE)
 
-        def score(c):
+        def interleaved(tile):
+            return tile[:].rearrange("p (n i t) -> p n t i", i=LINE, t=PACK)
+
+        def score(c, per_bank):
             z_words = stage.tile([P, CHUNK], U32, name="z_words", align_bytes=64)
             z_bytes = stage.tile([P, CHUNK], U8, name="z_bytes", align_bytes=64)
-            nc.vector.quantize_mx(out=z_words[:].bitcast(FP8X4), scales=z_bytes[:], in_=z_bf[c])
-            per_bank = 2 if c < CHUNKS - 2 else 1
-            for b in range(PACK // per_bank):
+            nc.vector.quantize_mx(out=z_words[:].bitcast(FP8X4), scales=z_bytes[:], in_=z_bf[c][:])
+            for m0 in range(0, CAND_BLOCKS, per_bank):
                 bank = psum.tile([P, per_bank, CHUNK], F32, name="out_bank", tag="bank")
                 for i in range(per_bank):
-                    rows = slice((per_bank * b + i) * P, (per_bank * b + i + 1) * P)
-                    nc.tensor.matmul_mx(out=bank[:, i, :], lhsT=cand_words[:, rows].bitcast(FP8X4), lhsT_scale=cand_bytes[:, rows],
-                                        rhs=z_words[:].bitcast(FP8X4), rhs_scale=z_bytes[:], start=True, stop=True)
-                result = stage.tile([P, per_bank, CHUNK], F32, name="result", bufs=8)
-                nc.scalar.activation(result[:], bank[:], COPY, scale=-0.0625)
-                nc.sync.dma_start(out_rows[:, per_bank * b : per_bank * (b + 1), c * CHUNK : (c + 1) * CHUNK], result[:])
+                    rows = slice((m0 + i) * P, (m0 + i + 1) * P)
+                    multiply(nc, bank[:, i, :], cand_words[:, rows], cand_bytes[:, rows], z_words[:], z_bytes[:])
+                result = stage.tile([P, per_bank, CHUNK], F32, name="result", bufs=BANKS)
+                nc.scalar.activation(result[:], bank[:], COPY, scale=OUT_FACTOR)
+                nc.sync.dma_start(out_blocks[:, m0 : m0 + per_bank, c * CHUNK : (c + 1) * CHUNK], result[:])
 
-        gather(0, range(PACK))
-        weave(0)
-        gather(1, range(PACK))
-        weave(1)
-        score(0)
-        gather(2, range(PACK))
-        weave(2)
-        score(1)
-        gather(3, range(3))
-        score(2)
-        gather(3, range(3, PACK))
-        c = CHUNKS - 1
-        src = diffs[c].rearrange("p (t n i) -> p n t i", t=PACK, i=4)
-        z_half = [keep.tile([P, span // 2], BF16, name=f"z_half{a}", align_bytes=64) for a in range(2)]
-        half_words = [keep.tile([P, CHUNK // 2], U32, name=f"half_words{a}", align_bytes=64) for a in range(2)]
-        half_bytes = [keep.tile([P, CHUNK // 2], U8, name=f"half_bytes{a}", align_bytes=64) for a in range(2)]
+        last = CHUNKS - 1
+        for c in range(last):
+            gather(c, range(PACK))
+            nc.scalar.copy(interleaved(z_bf[c]), by_lines(c))
+            if c > 0:
+                score(c - 1, per_bank=2)
+        gather(last, range(PACK - 1))
+        score(last - 1, per_bank=1)
+        gather(last, [PACK - 1])
+
+        half_c = CHUNK // 2
+        z_half = [keep.tile([P, SPAN // 2], BF16, name=f"z_half{a}", align_bytes=64) for a in range(2)]
+        half_words = [keep.tile([P, half_c], U32, name=f"half_words{a}", align_bytes=64) for a in range(2)]
+        half_bytes = [keep.tile([P, half_c], U8, name=f"half_bytes{a}", align_bytes=64) for a in range(2)]
         for a in range(2):
-            nc.vector.tensor_copy(z_half[a][:].rearrange("p (n i t) -> p n t i", i=4, t=PACK), src[:, a * (CHUNK // 8) : (a + 1) * (CHUNK // 8)])
+            nc.vector.tensor_copy(interleaved(z_half[a]), by_lines(last)[:, a * half_c // LINE : (a + 1) * half_c // LINE])
         for a in range(2):
             nc.vector.quantize_mx(out=half_words[a][:].bitcast(FP8X4), scales=half_bytes[a][:], in_=z_half[a][:])
-        banks = [psum.tile([P, CHUNK], F32, name=f"last_bank{m}", tag="bank") for m in range(PACK)]
+        banks = [psum.tile([P, CHUNK], F32, name=f"last_bank{m}", tag="bank") for m in range(CAND_BLOCKS)]
         for a in range(2):
-            for m in range(PACK):
+            for m in range(CAND_BLOCKS):
                 rows = slice(m * P, (m + 1) * P)
-                nc.tensor.matmul_mx(out=banks[m][:, a * (CHUNK // 2) : (a + 1) * (CHUNK // 2)], lhsT=cand_words[:, rows].bitcast(FP8X4), lhsT_scale=cand_bytes[:, rows],
-                                    rhs=half_words[a][:].bitcast(FP8X4), rhs_scale=half_bytes[a][:], start=True, stop=True)
-        for m in range(PACK):
-            result = stage.tile([P, 1, CHUNK], F32, name="result", bufs=8)
+                multiply(nc, banks[m][:, a * half_c : (a + 1) * half_c], cand_words[:, rows], cand_bytes[:, rows],
+                         half_words[a][:], half_bytes[a][:])
+        for m in range(CAND_BLOCKS):
+            result = stage.tile([P, 1, CHUNK], F32, name="result", bufs=BANKS)
             if m % 2 == 1:
-                nc.vector.tensor_scalar_mul(result[:, 0, :], banks[m][:], -0.0625)
+                nc.vector.tensor_scalar_mul(result[:, 0, :], banks[m][:], OUT_FACTOR)
             else:
-                nc.scalar.activation(result[:, 0, :], banks[m][:], COPY, scale=-0.0625)
-            nc.sync.dma_start(out_rows[:, m : m + 1, c * CHUNK : (c + 1) * CHUNK], result[:])
+                nc.scalar.activation(result[:, 0, :], banks[m][:], COPY, scale=OUT_FACTOR)
+            nc.sync.dma_start(out_blocks[:, m : m + 1, last * CHUNK :], result[:])

from contextlib import ExitStack

import concourse.mybir as mybir

K, T, S, H, C, U = 512, 2048, 512, 512, 512, 1024
FLOPS = 2 * K * H * S + 2 * K * C * U

F32 = mybir.dt.float32
BF16 = mybir.dt.bfloat16
I32 = mybir.dt.int32
U32 = mybir.dt.uint32
U16 = mybir.dt.uint16
U8 = mybir.dt.uint8
FP8X4 = mybir.dt.float8_e4m3fn_x4
COPY = mybir.ActivationFunctionType.Copy
SUBTRACT = mybir.AluOpType.subtract

P = 128
PACK = 4
QUADRANT = 32
GROUP = 16
LINE = 4
CHUNK = 256
CHUNKS = U // CHUNK
SPAN = PACK * CHUNK
CAND_BLOCKS = C // P
BANKS = 8
OUT_FACTOR = -0.0625
KIB = 1024

AT_DIFFS = 0
AT_LAST_PAGE = 8 * KIB
AT_W_SECOND = 12 * KIB


def multiply(nc, bank, lhs_words, lhs_bytes, rhs_words, rhs_bytes):
    nc.tensor.matmul_mx(out=bank, lhsT=lhs_words.bitcast(FP8X4), lhsT_scale=lhs_bytes,
                        rhs=rhs_words.bitcast(FP8X4), rhs_scale=rhs_bytes, start=True, stop=True)


def tile_picked_candpg_none_p_kernel(tc, x_words, x_scales, w1, mem, gs, offs, slot, mate, cand, out):
    nc = tc.nc
    with ExitStack() as ctx:
        lists = ctx.enter_context(tc.tile_pool(name="lists", bufs=1))
        keep = ctx.enter_context(tc.tile_pool(name="keep", bufs=1))
        shared = ctx.enter_context(tc.tile_pool(name="shared", bufs=1))
        stage = ctx.enter_context(tc.tile_pool(name="stage", bufs=CHUNKS))
        psum = ctx.enter_context(tc.psum_pool(name="psum", bufs=BANKS))

        offs_t = lists.tile([P, S // GROUP], U16, name="offs_t")
        cand_t = lists.tile([P, C // GROUP], U16, name="cand_t")
        slot_t = lists.tile([P, S // GROUP], U16, name="slot_t")
        mate_t = lists.tile([P, U // GROUP], U16, name="mate_t")
        table_words = keep.tile([P, T], I32, name="table_words")
        table_bytes = keep.tile([P, T], U8, name="table_bytes")
        w_raw = [keep.tile([P, PACK, H // 2], F32, name="w_first"),
                 shared.tile([P, PACK, H // 2], F32, name="w_second", offset=AT_W_SECOND, align_bytes=64)]
        gain = keep.tile([P, PACK], F32, name="gain")
        page = [keep.tile([P, U], F32, name=f"page{t}") for t in range(PACK - 1)]
        page.append(shared.tile([P, U], F32, name="page_last", offset=AT_LAST_PAGE, align_bytes=64))

        nc.vector.memset(table_bytes[:].bitcast(I32), 0)
        nc.sync.dma_start(offs_t[:], offs)
        nc.sync.dma_start(cand_t[:], cand)
        w_rows = w1.rearrange("(p j) c -> p j c", j=PACK)
        nc.sync.dma_start(w_raw[0][:], w_rows[:, :, : H // 2])
        scale_rows = x_scales[0].rearrange("(q r) n -> r q n", r=PACK)
        for r in range(PACK):
            nc.sync.dma_start(table_bytes[r:P:QUADRANT, :].bitcast(I32), scale_rows[r].bitcast(I32))
        nc.sync.dma_start(w_raw[1][:], w_rows[:, :, H // 2 :])
        nc.sync.dma_start(table_words[:], x_words[0].rearrange("p n j -> p (n j)").bitcast(I32))
        mem_planes = mem.rearrange("(p t) w -> p t w", t=PACK)
        nc.sync.dma_start(slot_t[:], slot)
        nc.sync.dma_start(page[0][:], mem_planes[:, 0, :])
        nc.sync.dma_start(gain[:], gs.rearrange("(p t) o -> p (t o)", t=PACK))
        for t in range(1, PACK):
            nc.sync.dma_start(page[t][:], mem_planes[:, t, :])
        nc.sync.dma_start(mate_t[:], mate)

        tok_words = shared.tile([P, S], U32, name="tok_words", offset=AT_W_SECOND, align_bytes=64)
        tok_bytes = keep.tile([P, S], U8, name="tok_bytes", align_bytes=64)
        cand_words = shared.tile([P, C], U32, name="cand_words", offset=AT_W_SECOND + 4 * S, align_bytes=64)
        cand_bytes = keep.tile([P, C], U8, name="cand_bytes", align_bytes=64)
        nc.vector.tensor_copy(tok_bytes[:], table_bytes[:].indirect(offs_t[:]))
        nc.vector.tensor_copy(cand_bytes[:], table_bytes[:].indirect(cand_t[:]))

        w_bf = keep.tile([P, H * PACK], BF16, name="w_bf", align_bytes=64)
        w_dealt = w_bf[:].rearrange("p (t m j) -> p m j t", t=PACK, j=PACK)
        for a in range(2):
            nc.scalar.copy(w_dealt[:, a * (P // 2) : (a + 1) * (P // 2), :, :], w_raw[a][:].rearrange("p j (m t) -> p m j t", t=PACK))
        w_words = keep.tile([P, H], U32, name="w_words", align_bytes=64)
        w_bytes = keep.tile([P, H], U8, name="w_bytes", align_bytes=64)
        h_planes = keep.tile([P, PACK, S], F32, name="h_planes")
        nc.vector.quantize_mx(out=w_words[:].bitcast(FP8X4), scales=w_bytes[:], in_=w_bf[:])

        half_s = S // 2
        for s0 in range(0, S, half_s):
            nc.vector.tensor_copy(tok_words[:, s0 : s0 + half_s],
                                  table_words[:].bitcast(U32).indirect(offs_t[:, s0 // GROUP : (s0 + half_s) // GROUP]))
        nc.vector.tensor_copy(cand_words[:], table_words[:].bitcast(U32).indirect(cand_t[:]))
        for t in range(PACK):
            cols = slice(t * P, (t + 1) * P)
            width = half_s if t == 0 else S
            for s0 in range(0, S, width):
                toks = slice(s0, s0 + width)
                h_bank = psum.tile([P, width], F32, name="h_bank", tag="bank")
                multiply(nc, h_bank[:], w_words[:, cols], w_bytes[:, cols], tok_words[:, toks], tok_bytes[:, toks])
                nc.scalar.copy(h_planes[:, t, toks], h_bank[:])

        window = [keep.tile([P, U], F32, name=f"window{t}") for t in range(PACK)]
        plain = []
        for t in range(PACK):
            weight = gain[:, t : t + 1]
            nc.vector.tensor_copy(page[t][:].indirect(slot_t[:]), h_planes[:, t, :])
            nc.scalar.activation(window[t][:], page[t][:], COPY, scale=weight)
            if t < PACK - 1:
                whole = keep.tile([P, U], F32, name=f"plain{t}")
                nc.scalar.activation(whole[:], page[t][:], COPY, scale=weight)
                plain.append([whole[:, c * CHUNK : (c + 1) * CHUNK] for c in range(CHUNKS)])
            else:
                first = keep.tile([P, CHUNK], F32, name="plain_first")
                nc.scalar.activation(first[:], page[t][:, :CHUNK], COPY, scale=weight)
                rest = keep.tile([P, U - CHUNK], F32, name="plain_rest")
                nc.scalar.copy(rest[:], window[t][:, CHUNK:])
                plain.append([first[:]] + [rest[:, c * CHUNK : (c + 1) * CHUNK] for c in range(CHUNKS - 1)])

        diff0 = shared.tile([P, SPAN], F32, name="diff0", offset=AT_DIFFS, align_bytes=64)
        diff1 = shared.tile([P, SPAN], F32, name="diff1", offset=AT_LAST_PAGE, align_bytes=64)
        diff23 = shared.tile([P, 2 * SPAN - CHUNK], F32, name="diff23", offset=AT_DIFFS, align_bytes=64)
        diffs = [diff0[:], diff1[:], diff23[:, SPAN - CHUNK :], diff23[:, :SPAN]]
        z_bf = [keep.tile([P, SPAN], BF16, name=f"z_bf{c}", align_bytes=64) for c in range(CHUNKS - 1)]
        out_blocks = out.rearrange("(m q) w -> q m w", q=P)

        def gather(c, planes):
            entries = mate_t[:, c * CHUNK // GROUP : (c + 1) * CHUNK // GROUP]
            for t in planes:
                nc.vector.tensor_tensor(diffs[c][:, t * CHUNK : (t + 1) * CHUNK], window[t][:].indirect(entries), plain[t][c], SUBTRACT)

        def by_lines(c):
            return diffs[c].rearrange("p (t n i) -> p n t i", t=PACK, i=LINE)

        def interleaved(tile):
            return tile[:].rearrange("p (n i t) -> p n t i", i=LINE, t=PACK)

        def score(c, per_bank):
            z_words = stage.tile([P, CHUNK], U32, name="z_words", align_bytes=64)
            z_bytes = stage.tile([P, CHUNK], U8, name="z_bytes", align_bytes=64)
            nc.vector.quantize_mx(out=z_words[:].bitcast(FP8X4), scales=z_bytes[:], in_=z_bf[c][:])
            for m0 in range(0, CAND_BLOCKS, per_bank):
                bank = psum.tile([P, per_bank, CHUNK], F32, name="out_bank", tag="bank")
                for i in range(per_bank):
                    rows = slice((m0 + i) * P, (m0 + i + 1) * P)
                    multiply(nc, bank[:, i, :], cand_words[:, rows], cand_bytes[:, rows], z_words[:], z_bytes[:])
                result = stage.tile([P, per_bank, CHUNK], F32, name="result", bufs=BANKS)
                nc.scalar.activation(result[:], bank[:], COPY, scale=OUT_FACTOR)
                nc.sync.dma_start(out_blocks[:, m0 : m0 + per_bank, c * CHUNK : (c + 1) * CHUNK], result[:])

        last = CHUNKS - 1
        for c in range(last):
            gather(c, range(PACK))
            nc.scalar.copy(interleaved(z_bf[c]), by_lines(c))
            if c > 0:
                score(c - 1, per_bank=2)
        gather(last, range(PACK - 1))
        score(last - 1, per_bank=1)
        gather(last, [PACK - 1])

        half_c = CHUNK // 2
        z_half = [keep.tile([P, SPAN // 2], BF16, name=f"z_half{a}", align_bytes=64) for a in range(2)]
        half_words = [keep.tile([P, half_c], U32, name=f"half_words{a}", align_bytes=64) for a in range(2)]
        half_bytes = [keep.tile([P, half_c], U8, name=f"half_bytes{a}", align_bytes=64) for a in range(2)]
        for a in range(2):
            nc.vector.tensor_copy(interleaved(z_half[a]), by_lines(last)[:, a * half_c // LINE : (a + 1) * half_c // LINE])
        for a in range(2):
            nc.vector.quantize_mx(out=half_words[a][:].bitcast(FP8X4), scales=half_bytes[a][:], in_=z_half[a][:])
        banks = [psum.tile([P, CHUNK], F32, name=f"last_bank{m}", tag="bank") for m in range(CAND_BLOCKS)]
        for a in range(2):
            for m in range(CAND_BLOCKS):
                rows = slice(m * P, (m + 1) * P)
                multiply(nc, banks[m][:, a * half_c : (a + 1) * half_c], cand_words[:, rows], cand_bytes[:, rows],
                         half_words[a][:], half_bytes[a][:])
        for m in range(CAND_BLOCKS):
            result = stage.tile([P, 1, CHUNK], F32, name="result", bufs=BANKS)
            if m % 2 == 1:
                nc.vector.tensor_scalar_mul(result[:, 0, :], banks[m][:], OUT_FACTOR)
            else:
                nc.scalar.activation(result[:, 0, :], banks[m][:], COPY, scale=OUT_FACTOR)
            nc.sync.dma_start(out_blocks[:, m : m + 1, last * CHUNK :], result[:])
